import numpy as np, ml_dtypes
CORES = [10,34,74,98]
N = 4
BF = ml_dtypes.bfloat16
def gentries(a):
    return np.ascontiguousarray(a.reshape(8, 16, -1).transpose(0, 2, 1)).reshape(8, -1)
def gtable(e):
    e = np.asarray(e); return np.ascontiguousarray(e.reshape(8, -1, 16).transpose(0, 2, 1)).reshape(128, -1).astype(np.int32)
V, G, CAP, D, P, RO = 2048, 256, 64, 4, 2048, 5
W = V + (N - 1) * G
def paths(rng, n):
    s = (N, 8, 16, V)
    q = np.where(rng.random(s) < 0.6, np.arange(N).reshape(N, 1, 1, 1), rng.integers(0, N, s))
    u = np.where(rng.random(s) < 0.6, (np.arange(V) + rng.integers(-8, 9, s)) % V, rng.integers(0, V, s))
    a = q * V + u + 1; a[:, :, 0] = (np.arange(N * V) + 1).reshape(N, 1, V)
    return np.where(np.arange(16).reshape(16, 1) < n, a, 0)
def parts(rng):
    s = (N, 8, D, V)
    n = np.where(rng.random((N, 8, 1, V)) < rng.choice(np.array([0.1, 0.3, 0.6]), (N, 8, 1, 1)), 0, rng.integers(1, 17, (N, 8, 1, V)))
    return {"path": paths(rng, n), "toll": rng.integers(0, 256, (N, 128, W)),
            "nb": np.where(rng.random(s) < 0.5, (np.arange(V) + rng.integers(-8, 9, s)) % V, rng.integers(0, W, s)),
            "pr": rng.integers(0, 16, s) % rng.choice(np.array([2, 4, 16]), (N, 8, 1, 1)),
            "dn": np.where(rng.random(s) < 0.75, 15, rng.integers(0, RO + 1, s)),
            "org": rng.random((N, 8, V)) < rng.choice(np.array([0.01, 0.05]), (N, 8, 1)),
            "shown": np.ascontiguousarray(np.argsort(rng.random((N, 8, N - 1, V)), axis=-1)[..., :G]),
            "at": rng.integers(0, W, (N, 8, P))}
def pack(d):
    return {"path0": np.ascontiguousarray(d["path"].reshape(N, 128, V)).astype(np.int32), "toll": d["toll"].astype(np.float32).astype(BF),
            "nb": np.stack([gtable(a.reshape(8, -1)) for a in d["nb"]]), "lk": (16 * d["dn"] + d["pr"]).reshape(N, 8, D * V).astype(np.int32),
            "org": d["org"].astype(np.int32), "shown": np.stack([gtable(a.reshape(8, -1)) for a in d["shown"]]), "at0": np.stack([gtable(a) for a in d["at"]])}
def setup_inputs(rng):
    return pack(parts(rng))
def late(rng, d, p, q, g):
    odd = 2 * rng.permutation(V // 2) + 1; even = 2 * rng.permutation(V // 2); u = V // 16
    x, y1, y3, f0, f1 = odd[:u], odd[u:2 * u], odd[2 * u:3 * u], odd[3 * u:3 * u + 16], odd[3 * u + 16:3 * u + 32]
    z0, z2 = even[:u], even[u:2 * u]
    quiet = np.concatenate([even[2 * u:3 * u], odd[3 * u + 32:4 * u + 32]]); rd = np.concatenate([even[3 * u:], odd[4 * u + 32:]])
    for k in (y1, y3, f1, z2, quiet): p[:, k] = 0
    p[8:, f0] = 0; p[1:, f0[:8]] = 0
    o = d["org"][q, g]; o[:] = False; o[f0] = True; o[f1] = True
    nb = d["nb"][q, g]; dn = d["dn"][q, g]
    for k, f, m in ((x, f0, (2, 15)), (y1, f0, (3, 15)), (y3, f1, (4, 15)), (z0, f0[:8], (15, 15)), (z2, f1, (3, 15)), (quiet, f0, (0, 0))):
        nb[:, k] = rng.choice(f, len(k)); dn[:, k] = rng.choice(np.array(m), len(k))
    nb[:, rd] = np.where(rng.random((D, len(rd))) < 0.75, rng.integers(V, W, (D, len(rd))), nb[:, rd])
    for e in range(N - 1):
        sc = (q + e + g // 2) % 4; m = CAP - 1 + (q + e) % 3; n = rng.integers(0, 4, 5)
        if sc == 0: n[0] = rng.integers(8, 20); n[1] = rng.integers(3, 7); n[2] = 0; n[3] = rng.integers(0, 2)
        if sc == 1: n[2] = m - n[1]
        if sc == 2: n[3] = m
        if sc == 3: n[1:3] = 0; n[4] = m
        a = np.concatenate([rng.choice(k, int(i)) for k, i in zip((z0, x, y1, z2, y3), n)])
        if sc > 0: a = rng.permutation(a)
        a = np.concatenate([rng.choice(quiet, G - len(a)), a])
        if sc > 0 and rng.random() < 0.5: a = rng.permutation(a)
        d["shown"][q, g, e] = a
def setup_inputs_room(rng):
    d = parts(rng); path = paths(rng, rng.integers(1, 17, (N, 8, 1, V))); odd = 2 * np.arange(V // 2) + 1; h = V // 4
    for q in range(N):
        for g in range(0, 8, 2):
            o = rng.permutation(odd); a, b = o[:h], o[h:]
            path[q, g][:, b] = 0
            for e in range(N - 1):
                n = int(rng.choice(np.array([0, 1, CAP - 1, CAP, CAP + 1, G])))
                if q < 2 and e == 0: n = ((CAP, CAP + 1, G, CAP - 1), (1, 0, CAP, CAP + 1))[q][g // 2]
                d["shown"][q, g, e] = rng.permutation(np.concatenate([rng.permutation(a)[:n], rng.permutation(b)[:G - n]]))
        for g in range(1, 8, 2): late(rng, d, path[q, g], q, g)
    d["path"] = path
    return pack(d)
def setup_inputs_ties(rng):
    d = parts(rng); s = (N, 8, D, V)
    path = paths(rng, rng.choice(np.array([1, 14, 15, 16]), (N, 8, 1, V)))
    d["pr"] = rng.choice(np.array([0, 7, 14]), (N, 8, 1, 1)) + rng.integers(0, 2, s) * rng.integers(0, 2, (N, 8, 1, 1))
    d["dn"] = rng.choice(np.array([0, 1, 2, RO - 1, RO, 15, 15, 15]), s)
    v = np.arange(1, V, 4); c = v + 2; j = np.arange(16).reshape(16, 1); z = len(v); x = np.arange(z); m = N * V // 2
    wt = np.array([1, 37, 101, 13, 89, 53, 127, 7, 71, 113, 29, 97, 61, 19, 109, 43])
    for q in range(N):
        for g in (1, 3, 5, 7):
            lo, hi = {1: (2, 15), 3: (2, 16), 5: (3, 15), 7: (8, 15)}[g]
            n = rng.integers(lo, hi, z); kd = rng.integers(0, 6, z); rim = 128 if g == 7 else 0
            if g == 3: n = np.where(kd == 5, 15, np.where(kd == 4, np.minimum(n, 14), n))
            a = 2 * rng.integers(rim, m - rim, (16, z)) + 1; a[0] = q * V + c + 1; a = np.where(j < n, a, 0)
            h = np.flatnonzero((kd == 4) & (x % 2 == 0))
            if g == 3: a[n[h] - 1, h] = N * V
            b = np.concatenate([a[:1], a[:15]])
            if g == 1:
                b = np.take_along_axis(a, np.clip(n - j, 0, 15), 0); b = np.where((j >= 1) & (j <= n), b, 0)
            elif g == 5:
                i = rng.integers(2, n); k = rng.integers(i + 1, n + 1)
                b[i, x] = a[k - 1, x]; b[k, x] = a[i - 1, x]
            elif g == 3:
                k = np.where(kd == 5, 15, rng.integers(1, n + 1))
                by = np.where(kd == 1, V * rng.integers(1, N, z), np.where(kd == 2, 2, np.where(kd == 3, 2 ** rng.integers(1, 13, z), 2 * rng.integers(1, m, z))))
                b[k, x] = np.where(kd == 4, b[k, x], (b[k, x] - 1 + by) % (N * V) + 1)
                b[n[h], h] = 0
                h = np.flatnonzero((kd == 4) & (x % 2 == 1)); b[n[h] + 1, h] = N * V
                h = np.flatnonzero(kd == 5)[::3]; b[15, h] = 0
            else:
                kd = kd % 3; o = np.argsort(np.where((j >= 2) & (j <= n), rng.random((16, z)), 2.0), axis=0)[:4]
                by = np.where(kd == 0, np.array([[2], [2], [-2], [-2]]), 0); w2 = 2 ** rng.integers(1, 7, (2, z))
                by[0] = np.where(kd == 1, w2[0], np.where(kd == 2, 2 * wt[o[1]], by[0]))
                by[1] = np.where(kd == 1, -w2[1], np.where(kd == 2, -2 * wt[o[0]], by[1]))
                b[o, x] = b[o, x] + by
            b[0] = q * V + v + 1
            path[q, g][:, c] = a; path[q, g][:, v] = b
            d["nb"][q, g][:, v] = c; d["dn"][q, g][:, v] = 15; d["org"][q, g, v] = False
            for e in range(N - 1): d["shown"][q, g, e] = rng.permutation(v)[:G]
    d["path"] = path
    return pack(d)
def setup_inputs_loops(rng):
    d = parts(rng); nb = d["nb"]; snd = d["shown"]
    for g in range(8): nb[N - 1, g, :, V - 1] = 2 * rng.permutation(V // 2 - 1)[:D] + 1
    d["dn"][N - 1, :, :, V - 1] = 15; d["org"][N - 1, :, V - 1] = False
    n = np.where(rng.random((N, 8, 1, V)) < 0.8, 15, rng.integers(1, 16, (N, 8, 1, V))); path = paths(rng, n)
    for q in range(N):
        for g in range(8):
            for i in range(D):
                v = np.flatnonzero((nb[q, g, i] < V) & (rng.random(V) < 0.3)); u = nb[q, g, i][v]
                who = np.where(rng.random(len(v)) < 0.7, q, (q + 1) % N)
                path[q, g][(rng.random(len(v)) * n[q, g, 0, u]).astype(np.int64), u] = who * V + v + 1
                for e in range(N - 1):
                    b = (q + e + 1) % N; k = nb[b, g, i] - V - e * G
                    v = np.flatnonzero((k >= 0) & (k < G) & (rng.random(V) < 0.5)); u = snd[q, g, e][k[v]]
                    path[q, g][(rng.random(len(v)) * n[q, g, 0, u]).astype(np.int64), u] = b * V + v + 1
    for g in range(8):
        u = nb[N - 1, g, :, V - 1]; path[N - 1, g][(rng.random(D) * n[N - 1, g, 0, u]).astype(np.int64), u] = N * V
    d["path"] = path
    return pack(d)
def setup_inputs_ends(rng):
    d = parts(rng); nb = d["nb"]
    d["shown"][:, ::2] = rng.choice(np.array([0, V - 1, V // 2, 3]), (N, 4, N - 1, G)); d["at"][:, ::2] = rng.choice(np.array([0, V - 1, V, W - 1]), (N, 4, P))
    nb[:, 0] = nb[:, 0, :1]; nb[:, 2] = rng.integers(V, W, (N, D, V)); nb[:, 4] = rng.integers(0, V, (N, D, V))
    nb[:, 6] = rng.choice(np.array([0, V - 1, V, W - 1]), (N, D, V))
    d["path"][:, 3] = 0; d["org"][:, 3] = False
    d["path"][:, 1] = 0; d["org"][:, 1] = False; d["org"][0, 1, V - 1] = True
    d["org"][:, 5] = True; d["dn"][:, 7] = 0; d["toll"][:, :, ::3] = 255
    return pack(d)
def setup_inputs_spread(rng):
    d = parts(rng); s = (N, 8, D, V)
    n = np.minimum(np.exp2(4.2 * rng.random((N, 8, 1, V))).astype(np.int64) - 1, 16)
    a = np.minimum(np.exp2(13 * rng.random((N, 8, 16, V))).astype(np.int64), N * V)
    d["path"] = np.where(np.arange(16).reshape(16, 1) < n, a, 0)
    d["nb"] = rng.integers(0, W, s); d["pr"] = rng.integers(0, 16, s); d["dn"] = rng.integers(0, 16, s)
    d["org"] = rng.random((N, 8, V)) < np.exp2(-8 * rng.random((N, 8, 1))); d["shown"] = rng.integers(0, V, (N, 8, N - 1, G))
    d["toll"] = np.minimum((np.exp2(8 * rng.random((N, 1, W))) * rng.random((N, 128, W))).astype(np.int64), 255)
    d["at"] = np.minimum((W * rng.random((N, 8, P)) ** 3).astype(np.int64), W - 1)
    return pack(d)
def check_inputs(d):
    bad = []
    for k, hi in (("path0", N * V), ("nb", W - 1), ("lk", 255), ("org", 1), ("shown", V - 1), ("at0", W - 1)):
        if np.min(d[k]) < 0 or np.max(d[k]) > hi: bad.append("range of " + k)
    t = d["toll"].astype(np.float32)
    if not np.all((t >= 0) & (t <= 255) & (t == np.floor(t))): bad.append("toll: whole numbers from 0 to 255")
    p = d["path0"].reshape(-1, 16, V)
    if np.any((p[:, :15] == 0) & (p[:, 1:] != 0)): bad.append("filled rows of path0 come first")
    return bad
def reference(path0, toll, nb, lk, org, shown, at0):
    A = np.zeros((N, 8, 16, W), np.int32); A[..., :V] = path0.reshape(N, 8, 16, V)
    nbl = np.stack([gentries(a) for a in nb]).astype(np.int64).reshape(N, 8, D, V)
    sl = np.stack([gentries(a) for a in shown]).astype(np.int64).reshape(N, 8, N - 1, G)
    pos = [gentries(a).astype(np.int64) for a in at0]
    pr = (lk & 15).reshape(N, 8, D, V); dn = (lk >> 4).reshape(N, 8, D, V)
    fee = toll.astype(np.float32).astype(np.int32).reshape(N, 8, 16, W); S = np.zeros((N, 8, 16, P), np.int32)
    me = np.arange(V, dtype=np.int64); rest = np.broadcast_to(np.arange(V, W, dtype=np.int64), (8, W - V))
    for t in range(RO):
        for r in range(N):
            name = (r * V + me + 1).astype(np.int32)
            c = np.take_along_axis(A[r], nbl[r].reshape(8, 1, D * V), 2).reshape(8, 16, D, V)
            length = np.add.reduce((c > 0).astype(np.int32), axis=1)
            ok = (t < dn[r]) & (c[:, 0] > 0) & (c[:, 15] == 0) & ~np.any(c == name, axis=1)
            w = np.argmax(np.where(ok, 32 * pr[r] + 16 - length, -1), axis=1)
            some = np.any(ok, axis=1) & (org[r] == 0)
            best = np.take_along_axis(c, w[:, None, None, :], 2)[:, :, 0]
            new = np.zeros((8, 16, V), np.int32)
            new[:, 0] = np.where(some | (org[r] == 1), name, 0); new[:, 1:] = np.where(some[:, None], best[:, :15], 0)
            nh = np.where(some, np.take_along_axis(nbl[r], w[:, None], 1)[:, 0], me)
            A[r, :, :, (t & 1):V:2] = new[:, :, (t & 1)::2]
            pos[r] = np.take_along_axis(np.concatenate([nh, rest], axis=1), pos[r], 1)
            S[r] = (S[r] + np.take_along_axis(fee[r], pos[r][:, None], 2)) & 255
        for q in range(N):
            for d in range(1, N):
                b = (q + d) % N; lo = V + (d - 1) * G
                cur = np.take_along_axis(A[q], sl[q, :, d - 1][:, None], 2); old = A[b, :, :, lo:lo + G].copy()
                ch = np.any(cur != old, axis=1).astype(np.int64); before = np.add.accumulate(ch, axis=1) - ch
                A[b, :, :, lo:lo + G] = np.where(((ch == 1) & (before < CAP))[:, None], cur, old)
    return {"ypath": A[..., :V].reshape(N, 128, V).astype(np.float32), "ysum": S.reshape(N, 128, P).astype(np.float32).astype(BF)}

import math
from concourse.bass import DstId, RemoteDMATransfer
from concourse.mybir import AluOpType as ALU, ActivationFunctionType as AF

N, V, HV, G, G3, RO, W = 4, 2048, 1024, 256, 768, 5, 2816
OWN, GH, SP, TW = 768, 2816, 3584, 3600
A = 0.0088
B0 = 9 * math.log(2.0)
KD = 3230
SIG = math.exp(-B0 - KD * A)
MAGIC = 12582912.0
BIG = 8192.0
OFF = 64.5 * BIG
EQ, MUL, ADD, MAX, MIN, AND = ALU.is_equal, ALU.mult, ALU.add, ALU.max, ALU.min, ALU.bitwise_and

SCRATCH = {"lki": ("sbuf", [128, 8, 64], "int32"), "ori": ("sbuf", [128, 8, 32], "int32")}
for _d, _l in (
        ("int32", "p0i:2048 nbi:512 shi:48 ati:128 ls:512 dni:512 pri:512 m1:64 m1a:64 mi:128 mia:128 u1:2816 h0:2816 pci:8"),
        ("float32", "p0f:2048 nbf:512 base:512 defx:128 defs:128 sa:48 sb:48 smask:48 y1:48 nmf:2048 mr1:64 mr2:64 u4:2816 u3:2816 "
                    "u2:2816 col:32 xx:144 xg:128 idf:128 sel0:144 sel1:144 ta:128 tb:128 tc:128 td:128 te:128 tf:32"),
        ("bfloat16", "p0x:2048 p0s:2048 lkb:512 orb:256 tl:2816 tl2:2048 dnb:512 pen:2560 chg:48 cum:48 nm:2048 ne:2048 c1:4096 e1:4096 "
                     "c2:4096 e2:4096 wn:1024 dif:768 ones:768 ys:2048 idb:128 idp:128 i15:128 bo:144 bc:144 be:144 shf:128 wi:128 "
                     "a1:128 a2:128 tab0:3600 tab1:3600 tab2:3600 tab3:3600 tab4:3600 tab5:3600"),
        ("uint16", "lnk:512 shl:48 atl:128 pl:64 sel:48 nhl:640")):
    for _e in _l.split():
        SCRATCH[_e.split(":")[0]] = ("sbuf", [128, int(_e.split(":")[1])], _d)
for _b in ("k0", "k1", "k2", "k3", "n0", "n1", "n2", "n3"):
    SCRATCH[_b] = ("psum", [128, 512], "float32")

SEMAPHORES = "qv qa qp qg sent dnn dlk dor dsh dat dtl dt2 dp0 dp1 dp2 dp3 dout arr0 arr1 arr2 arr3".split()


def rank_program(g, core, T, topo):
    rank = T.rank_of(core)
    if rank is None:
        return
    ops = []

    def rec(q, fn, r="", w="", x="", dma=None, ext=()):
        ops.append({"q": q, "fn": fn, "r": r.split(), "w": w.split(), "x": x.split(), "dma": dma, "ext": list(ext)})

    def ts(out, in0, s1, s2, op0, op1, r, w, x=""):
        if op1 is None:
            rec("v", lambda: g.vector.tensor_scalar(out, in0, s1, None, op0), r, w, x)
        else:
            rec("v", lambda: g.vector.tensor_scalar(out, in0, s1, s2, op0, op1), r, w, x)

    def tt(out, in0, in1, op, r, w, x="", ext=()):
        rec("v", lambda: g.vector.tensor_tensor(out, in0, in1, op), r, w, x, None, ext)

    def cp(out, in_, r, w, x=""):
        rec("v", lambda: g.vector.tensor_copy(out, in_), r, w, x)

    def act(out, in_, func, r, w, x="", bias=0.0, scale=1.0, ext=()):
        rec("a", lambda: g.scalar.activation(out, in_, func, bias=bias, scale=scale), r, w, x, None, ext)

    def mm(bank, out, lhsT, rhs, start, stop, r):
        rec("p", lambda: g.tensor.matmul(out, lhsT, rhs, start, stop), r, "", bank)

    def iota(out, pat, base, w):
        rec("g", lambda: g.iota(out, pat, base, 0, allow_small_or_imprecise_dtypes=True), "", w)

    def pcopy(out, in_, n, r, w):
        rec("g", lambda: g.affine_select(out, in_, [[1, n]], ALU.is_ge, 0.0, 0, 0), r, w)

    def dma(q, out, in_, sem, r, w):
        eng = g.sync if q == "s" else g.scalar
        rec(q, lambda: eng.dma_start(out, in_), r, w, "", sem)

    def ks(name, a, n):
        return " ".join("%s%d" % (name, j) for j in range(a, a + n))

    def sl(j, n, m=1):
        return slice(j * n, (j + m) * n)

    tab = [T["tab%d" % t] for t in range(RO + 1)]
    xx, x8 = T.xx[:], T.xx[:, 0:128]

    dma("s", T.nbi[:], T.nb[:], "dnn", "", "nbi")
    for c in range(4):
        dma("a", T.p0i[:, sl(c, 512)], T.path0[:, sl(c, 512)], "dp%d" % c, "", "p0i%d" % c)
    for k in range(8):
        dma("s", T.lki[:, k, :], T.lk[k], "dlk", "", "lki%d" % k)
    for k in range(8):
        dma("s", T.ori[0:64, k, :], T.org[k], "dor", "", "ori%d" % k)
    dma("s", T.shi[:], T.shown[:], "dsh", "", "shi")

    rec("g", lambda: g.iota(T.pci[:, 0:1], [[0, 1]], 0, 1), "", "pc0")
    iota(xx, [[1, 144]], 0, "xx")
    iota(T.nmf[:, 0:HV], [[2, HV]], rank * V + 1, "nmf0")
    iota(T.xg[:], [[16, 8], [0, 16]], 0, "xg")
    iota(T.defs[:], [[1, 2], [32, 64]], 4096, "defs")
    iota(T.nmf[:, HV:V], [[2, HV]], rank * V + 2, "nmf1")
    iota(T.sb[:], [[16, 48]], 0, "sb")
    iota(T.smask[:], [[0, 3], [1, 16]], 0, "smask")
    (cP, cR, cG, cS, cPAR, cG15, cC, cE, cT1, cZ, cSEL, cP0, cW, cIB, cBN, cBP, c15, cNE, cX0, cX1, cR2, cM15,
     cW1) = [T.col[:, j:j + 1] for j in range(23)]
    rec("v", lambda: g.vector.memset(T.ones[:], 1.0), "", "ones")
    rec("v", lambda: g.vector.memset(cBP, B0), "", "cBP")
    ts(T.pci[:, 1:2], T.pci[:, 0:1], 15, None, AND, None, "pc0", "pc1")
    ts(T.pci[:, 2:3], T.pci[:, 0:1], 112, None, AND, None, "pc0", "pc2")
    ts(T.pci[:, 3:4], T.pci[:, 0:1], 15, 1, AND, ALU.logical_shift_right, "pc0", "pc3")
    ts(T.pci[:, 4:5], T.pci[:, 0:1], 1, None, AND, None, "pc0", "pc4")
    cp(T.col[:, 0:5], T.pci[:, 0:5], ks("pc", 0, 5), "c")
    ts(cBN, cR, 15.0, -300.0, EQ, MUL, "c", "cBN")
    ts(cSEL, cG, cS, 8.0, ADD, ADD, "c", "cSEL")
    ts(cP0, cPAR, 0.0, None, EQ, None, "c", "cP0")
    ts(cG15, cG, 15.0, None, ADD, None, "c", "cG15")
    ts(cW, cR, 0.0, -529.0, EQ, MUL, "c", "cW")
    ts(cW1, cR, 15.0, None, ALU.is_lt, None, "c", "cW1")
    ts(cIB, cR, 15.0, 513.0, EQ, MUL, "c", "cIB")
    ts(cBN, cBN, cBP, None, ADD, None, "cBN cBP", "cBN")
    ts(T.idb[:], x8, cP, None, EQ, None, "c xx", "idb")
    ts(T.sel0[:], xx, cSEL, cP0, EQ, MUL, "cSEL cP0 xx", "sel0")
    ts(T.sel1[:], xx, cSEL, cPAR, EQ, MUL, "cSEL c xx", "sel1")
    ts(cW, cW, cW1, None, ADD, None, "cW cW1", "cW")
    ts(cIB, cIB, -512.0, None, ADD, None, "cIB", "cIB")
    ts(T.ta[:], x8, cP, 512.0, EQ, MUL, "c xx", "ta")
    ts(T.tb[:], x8, cG15, cW, EQ, MUL, "cG15 cW xx", "tb")
    ts(cC, cR, 15.0, -16384.0, EQ, MUL, "c", "cC")
    ts(cE, cR, 15.0, -16777216.0, ALU.is_lt, MUL, "c", "cE")
    ts(c15, cR, 15.0, None, EQ, None, "c", "c15")
    ts(cM15, cR, 15.0, 512.0, EQ, MUL, "c", "cM15")
    ts(cX0, cR, 14.0, 512.0, EQ, MUL, "c", "cX0")
    ts(cX1, cR, 15.0, -16.0, EQ, MUL, "c", "cX1")
    tt(T.wi[:], T.ta[:], T.tb[:], ADD, "ta tb", "wi")
    act(T.nm[:, 0:HV], T.nmf[:, 0:HV], AF.Exp, "nmf0 cBN", "nm0", "", cBN, A)
    ts(T.bc[:], xx, cG15, cC, EQ, MUL, "cG15 cC xx", "bc")
    ts(T.be[:], xx, cG15, cE, EQ, MUL, "cG15 cE xx", "be")
    ts(T.idf[:], x8, cP, None, EQ, None, "c xx", "idf")
    ts(T.idp[:], x8, cP, -16777216.0, EQ, MUL, "c xx", "idp")
    ts(tab[0][:, GH:SP], T.ones[:], cM15, None, MUL, None, "ones cM15", "T0.gh")
    ts(T.tf[:, 0:16], T.xx[:, 0:16], 0.0, cX0, EQ, MUL, "xx cX0", "tf0")
    ts(T.tf[:, 16:32], T.xx[:, 0:16], 1.0, cX1, EQ, MUL, "xx cX1", "tf1")
    ts(cT1, cP, 1.0, cG15, ADD, MIN, "c cG15", "cT1")
    ts(cZ, cR, 15.0, -(2.0 ** 99), EQ, MUL, "c", "cZ")
    ts(cNE, cR, 0.0, 2.0 ** 99, ALU.is_gt, MUL, "c", "cNE")
    ts(cR2, cR, 2.0, None, MUL, None, "c", "cR2")
    ts(cZ, cZ, 2.0 ** 15, None, MUL, None, "cZ", "cZ")
    ts(cNE, cNE, 2.0 ** 21, None, MUL, None, "cNE", "cNE")

    cp(T.nbf[:], T.nbi[:], "nbi", "nbf")
    tt(tab[0][:, SP:TW], T.tf[:, 0:16], T.tf[:, 16:32], ADD, "tf0 tf1", "T0.sp")
    for p in range(2):
        for h in range(2):
            mm("k0", T.k0[:, sl(p, 256)], T["sel%d" % p][:, 8 - 8 * h:136 - 8 * h], T.nbf[:, h:512:2], h == 0, h == 1, "sel0 sel1 nbf")

    def names_to_psum(p):
        for h in range(2):
            b = "n%d" % (2 * p + h)
            mm(b, T[b][:], T.idb[:], T.nm[:, sl(2 * p + h, 512)], True, True, "idb nm%d" % p)

    names_to_psum(0)

    def enc1(c):
        s = sl(c, 512)
        cp(T.p0f[:, s], T.p0i[:, s], "p0i%d" % c, "p0f%d" % c)
        act(T.p0x[:, s], T.p0f[:, s], AF.Exp, "p0f%d cBP" % c, "p0x%d" % c, "", cBP, A)

    def enc2(c):
        s, bank = sl(c, 512), ("n2", "n3", "k3", "n2")[c]
        ts(T.p0s[:, s], T.p0x[:, s], 513.0, None, ALU.is_gt, None, "p0x%d" % c, "p0s%d" % c)
        mm(bank, T[bank][:], T.idb[:], T.p0x[:, s], True, False, "idb p0x%d" % c)
        mm(bank, T[bank][:], T.wi[:], T.p0s[:, s], False, True, "wi p0s%d" % c)

    def enc3(c):
        bank = ("n2", "n3", "k3", "n2")[c]
        act(tab[0][:, OWN + c * 512:OWN + (c + 1) * 512], T[bank][:], AF.Identity, "cIB", "T0.own%d" % c, bank, cIB, 1.0)

    enc1(0)
    enc1(1)
    cp(T.lnk[:], T.k0[:], "", "lnk", "k0")
    for f, c in ((enc2, 0), (enc1, 2), (enc2, 1), (enc3, 0), (enc1, 3), (enc2, 2), (enc3, 1), (enc2, 3), (enc3, 2), (enc3, 3)):
        f(c)

    for j in range(4):
        cp(T.lkb[:, sl(j, 128)], T.lki[:, :, 32 * (j % 2) + j // 2:32 * (j % 2) + 32:2], ks("lki", 0, 8), "lkb%d" % j)
        mm("k1", T.k1[:, sl(j, 128)], T.lkb[:, sl(j, 128)], T.idb[:], True, True, "idb lkb%d" % j)
    for p in range(2):
        cp(T.orb[0:64, sl(p, 128)], T.ori[0:64, :, p:32:2], ks("ori", 0, 8), "orb%d" % p)
        mm("k2", T.k2[:, sl(p, 64)], T.orb[0:64, sl(p, 128)], T.idp[0:64, 0:64], True, True, "idp orb%d" % p)
    dma("s", T.ati[:], T.at0[:], "dat", "lkb3", "ati")
    dma("s", T.tl[:], T.toll[:], "dtl", "lkb3", "tl")
    dma("s", T.tl2[:], T.toll[:, 0:V], "dt2", "lkb3", "tl2")
    for j in range(4):
        cp(T.ls[:, (j // 2) * 256 + j % 2:(j // 2 + 1) * 256:2], T.k1[:, sl(j, 128)], "", "ls%d" % j, "k1")
    ts(T.defx[:], T.k2[:, 0:128], -(2.0 ** -24), float(SP - OWN), MUL, ADD, "", "defx", "k2")
    ts(T.pri[:], T.ls[:], 15, None, AND, None, ks("ls", 0, 4), "pri")
    ts(T.dni[:], T.ls[:], 4, None, ALU.logical_shift_right, None, ks("ls", 0, 4), "dni")
    for j in range(8):
        ts(T.base[:, sl(j, 64)], T.pri[:, sl(j, 64)], 524288.0, float((3 - j % 4) * 4096), MUL, ADD, "pri", "base%d" % j)
    for j in range(8):
        tt(T.dnb[:, sl(j, 64)], T.dni[:, sl(j, 64)], T.k2[:, sl(j // 4, 64)], ADD, "dni", "dnb%d" % j, "k2")
    tt(T.base[:], T.base[:], T.k0[:], ADD, ks("base", 0, 8), "base", "k0")
    ts(T.pen[:, 0:512], T.dnb[:], 0.0, None, ALU.is_le, None, ks("dnb", 0, 8), "pen0")

    def late_a():
        ts(T.i15[:], x8, cP, c15, EQ, MUL, "c c15 xx", "i15")
        ts(T.tc[:], x8, cT1, None, EQ, None, "cT1 xx", "tc")
        ts(T.td[:], x8, cG, cZ, EQ, MUL, "c cZ xx", "td")
        tt(T.shf[:], T.tc[:], T.td[:], ADD, "tc td", "shf")

    def late_b():
        ts(T.ne[:, 0:HV], T.nm[:, 0:HV], cNE, None, MAX, None, "nm0 cNE", "ne0")
        ts(T.bo[:], xx, cG15, None, EQ, None, "cG15 xx", "bo")
        cp(T.shl[:], T.shi[:], "shi", "shl")
        ts(tab[1][:, 0:G3], T.ones[:], cM15, None, MUL, None, "ones cM15", "T1.M1 T1.M2 T1.M3")

    def late_c():
        ts(T.a1[:], T.xg[:], cG, -BIG, EQ, MUL, "c xg", "a1")
        ts(T.te[:], x8, cP, -1.0, ALU.is_lt, MUL, "c xx", "te")
        ts(T.smask[:], T.smask[:], 1.0, None, MIN, None, "smask", "smask")
        ts(T.sa[:], T.shi[:], OWN - OFF, None, ADD, None, "shi", "sa")
        ts(T.sb[:], T.sb[:], cR, -OFF, ADD, ADD, "sb c", "sb")
        tt(T.a2[:], T.te[:], T.a1[:], MUL, "te a1", "a2")
        ts(T.defs[:], T.defs[:], cR2, None, ADD, None, "defs cR2", "defs")

    def own(t):
        return ks("T0.own", 0, 4) if t == 0 else "T%d.own" % t

    def win(t):
        return own(t) + " T%d.sp" % t + (" T0.gh " if t == 0 else " ")

    def arrived(t):
        return [("arr%d" % (t - 1), 16)] if t > 0 else []

    def links(t, p, j, n):
        return tab[t][:, OWN:TW].indirect(T.lnk[:, p * 256 + j * 32:p * 256 + (j + n) * 32])

    def gat_a(t, p, z, j, n):
        act(T["c" + z][:, sl(j, 512, n)], links(t, p, j, n), AF.Copy, win(t) + "lnk", ks("c%s." % z, j, n), "", 0.0, 1.0, arrived(t))

    def cmp_a(p, z, j, n):
        for a in range(j, j + n):
            bank = "n%d" % (2 * p + a % 2)
            tt(T["e" + z][:, sl(a, 512)], T["c" + z][:, sl(a, 512)], T[bank][:], EQ, "c%s.%d" % (z, a), "e%s.%d" % (z, a), bank)

    def gat_d(t, p, z):
        tt(T["c" + z][:, sl(3, HV)], links(t, p, 6, 2), T.nm[:, sl(p, HV)], ALU.subtract, win(t) + "lnk nm%d" % p, ks("c%s." % z, 6, 2), "",
           arrived(t))

    def eq_d(z):
        ts(T["e" + z][:, sl(3, HV)], T["c" + z][:, sl(3, HV)], 0.0, None, EQ, None, ks("c%s." % z, 6, 2), ks("e%s." % z, 6, 2))

    def fold_b(t, p, i, n, bank):
        o = p * 256 + i * 64
        mm(bank, T[bank][:, 0:n * 64], T.idf[:], T.base[:, o:o + n * 64], True, False, "idf base")
        mm(bank, T[bank][:, 0:n * 64], T.idp[:], T.pen[:, t * 512 + o:t * 512 + o + n * 64], False, False, "idp pen%d" % t)

    def fold(kind, z, i, n, bank):
        for k in range(16):
            mm(bank, T[bank][:, 0:n * 64], T["b" + kind][:, 15 - k:143 - k], T[kind + z][:, i * HV + k:(i + n) * HV:16], False,
               kind == "e" and k == 15, "b%s " % kind + ks("%s%s." % (kind, z), 2 * i, 2 * n))

    def mx(out, okey, bank, a, in1, ikey):
        tt(out, T[bank][:, sl(a, 64)], in1, MAX, ikey, okey, bank)

    def pick(q, out, in_, r, w):
        if q == "v":
            cp(out, in_, r, w)
        else:
            act(out, in_, AF.Copy, r, w)

    def path_gather(t, c, q):
        pick(q, T.wn[:, sl(c, G)], tab[t][:, OWN:TW].indirect(T.pl[:, sl(c, 16)]), win(t) + "pl", "wn%d" % c)

    def path_shift(c):
        bank = "k%d" % c
        mm(bank, T[bank][:, 0:G], T.i15[:], T.ones[:, 0:G], True, False, "i15 ones")
        mm(bank, T[bank][:, 0:G], T.shf[:], T.wn[:, sl(c, G)], False, True, "shf wn%d" % c)

    def path_put(t, p, c):
        bank = "k%d" % c
        tt(tab[t + 1][:, OWN + 2 * c * G + p:OWN + 2 * (c + 1) * G:2], T[bank][:, 0:G], T.ne[:, sl(4 * p + c, G)], MIN, "ne%d" % p,
           "T%d.own" % (t + 1), bank)

    def send(t, ds):
        def fn():
            trs = []
            for a, d in enumerate(ds):
                dst = T.cores[(rank + d) % N]
                eng = topo.engines(core, dst)
                k = len(eng) // len(ds)
                rid, pid, _ = topo.addr(dst)
                trs.append(RemoteDMATransfer(dst_ids=[DstId(rid=rid, pnc=pid)], dma_engine_mask=sum(1 << e for e in eng[sl(a, k)]),
                                             remote_sem=T.sem["arr%d" % t], src=tab[t + 2][:, sl(d - 1, G)],
                                             dst=tab[t + 1][:, GH + (d - 1) * G:GH + d * G]))
            return g.remote_dma_fused(trs, local_sem=T.sem.sent)
        rec("g", fn, " ".join("T%d.M%d" % (t + 2, d) for d in ds))

    def winners(p):
        mx(T.m1[:], "m1", "k3", 0, T.mr1[:], "mr1")

    def hops1(p):
        tt(T.mi[:, sl(p, 64)], T.m1[:], T.defs[:, sl(p, 64)], MAX, "m1 defs", "mi%d" % p)

    def hops2():
        ts(T.mia[:], T.mi[:], 4095, None, AND, None, "mi0 mi1", "mia")

    def hops3(t):
        cp(T.nhl[:, sl(t, 128)], T.mia[:], "mia", "nhl%d" % t)

    def half(t, p, z, mr, mk, dflt, dkey, after, gap):
        for i in range(4):
            fold_b(t, p, (i + 3) % 4, 1, "k%d" % i)
        if z == "1":
            gat_a(t, p, z, 0, 2)
        if t == 0:
            gat_a(t, p, z, 6, 2)
            cmp_a(p, z, 0, 2)
            cmp_a(p, z, 6, 2)
        else:
            if z == "1":
                gat_d(t, p, z)
            eq_d(z)
            cmp_a(p, z, 0, 2)
        gat_a(t, p, z, 2, 2)
        fold("c", z, 0, 1, "k1")
        fold("c", z, 3, 1, "k0")
        fold("e", z, 3, 1, "k0")
        fold("e", z, 0, 1, "k1")
        gat_a(t, p, z, 4, 1)
        gat_a(t, p, z, 5, 1)
        fold("c", z, 1, 1, "k2")
        cmp_a(p, z, 2, 2)
        mx(mr, mk, "k0", 0, dflt, dkey)
        cmp_a(p, z, 4, 1)
        fold("e", z, 1, 1, "k2")
        fold("c", z, 2, 1, "k3")
        after()
        mx(mr, mk, "k1", 0, mr, mk)
        cmp_a(p, z, 5, 1)
        fold("e", z, 2, 1, "k3")
        mx(mr, mk, "k2", 0, mr, mk)
        gap()

    chain = ["tl", "u4", "u3", "u2", "u1", "h0"]

    def back(j, p):
        t, src, dst = RO - 1 - j, chain[j], chain[j + 1]
        sk = "tl2 nhl%d " % t + ("%sg %s.0 %s.1" % (src, src, src) if j else "tl")
        gi = T[src][:, 0:W].indirect(T.nhl[:, sl(2 * t + p, 64)])
        if t > 0:
            tt(T[dst][:, p:V:2], gi, T.tl2[:, p:V:2], ADD, sk, "%s.%d" % (dst, p))
        else:
            ts(T[dst][:, p:V:2], gi, 255, None, AND, None, sk, "%s.%d" % (dst, p))

    for t in range(RO):
        p = t & 1
        q = 1 - p
        if t == 0:
            for u in range(1, RO):
                pcopy(tab[u][:, SP:TW], tab[0][:, SP:TW], 16, "T0.sp", "T%d.sp" % u)
        pcopy(tab[t + 1][:, OWN + q:GH:2], tab[t][:, OWN + q:GH:2], HV, own(t), "T%d.own" % (t + 1))

        def after():
            if t == 0:
                act(T.nm[:, HV:V], T.nmf[:, HV:V], AF.Exp, "nmf1 cBN", "nm1", "", cBN, A)
            else:
                gat_a(t, q, "2", 0, 2)

        def gap():
            if t == 0:
                late_a()
            else:
                hops2()
            if t == 1:
                ts(T.ne[:, HV:V], T.nm[:, HV:V], cNE, None, MAX, None, "nm1 cNE", "ne1")
            if t == 2:
                cp(T.atl[:], T.ati[:], "ati", "atl")
            if 0 < t:
                hops3(t - 1)
            if t == RO - 1:
                gat_d(t, q, "2")

        half(t, p, "1", T.mr1[:], "mr1", T.defx[:, sl(p, 64)], "defx", after, gap)
        dq = T.defs[:, sl(q, 64)]
        winners(p)
        ts(T.m1a[:], T.m1[:], 4095, None, AND, None, "m1", "m1a")
        cp(T.pl[:], T.m1a[:], "m1a", "pl")
        if t < RO - 1:
            for c in range(4):
                path_gather(t, c, "v" if c == 0 else "a")
                path_shift(c)
            if t == 0:
                names_to_psum(1)
                late_b()
                gat_a(t, q, "2", 0, 2)
            for c in range(4):
                path_put(t, p, c)
            gat_a(t, q, "2", 2, 2)
            if t > 0:
                gat_a(t, q, "2", 4, 2)
            nw = "T%d.own T%d.M1 T%d.M2 T%d.M3 " % ((t + 1,) * 4)
            tt(T.dif[:], tab[t + 1][:, OWN:GH].indirect(T.shl[:]), tab[t + 1][:, 0:G3], ALU.not_equal, nw + "shl", "dif")
            for k in range(16):
                mm("k0", T.k0[:, 0:48], T.bo[:, 15 - k:143 - k], T.dif[:, k:G3:16], k == 0, k == 15, "bo dif")
            if t == 0:
                late_c()
            else:
                cmp_a(q, "2", 0, 1)
            ts(T.chg[:], T.k0[:, 0:48], 1.0, None, MIN, None, "", "chg", "k0")
            rec("v", lambda: g.vector.tensor_tensor_scan(T.cum[:], T.smask[:], T.chg[:], 0.0, MUL, ADD), "smask chg", "cum")
            mm("k1", T.k1[:, 0:48], T.a2[:], T.chg[:], True, False, "a2 chg")
            mm("k1", T.k1[:, 0:48], T.a1[:], T.cum[:], False, True, "a1 cum")
            hops1(p)
            tt(T.y1[:], T.k1[:, 0:48], T.sb[:], MAX, "sb", "y1", "k1")
            tt(T.y1[:], T.y1[:], T.sa[:], MIN, "y1 sa", "y1")
            ts(T.sel[:], T.y1[:], OFF, None, ADD, None, "y1", "sel")
            for d, e in ((1, "a"), (2, "v"), (3, "a")):
                pick(e, tab[t + 2][:, sl(d - 1, G)], tab[t + 1][:, 0:GH].indirect(T.sel[:, sl(d - 1, 16)]), nw + "sel", "T%d.M%d" % (t + 2, d))
            send(t, (1, 2))
            send(t, (3,))
            if t == 0:
                gat_a(t, q, "2", 4, 2)
            gat_a(t, q, "2", 6, 2)
            fold_b(t, q, 0, 2, "k2")
            fold("c", "2", 0, 2, "k2")
            cmp_a(q, "2", min(t, 1), 4 - min(t, 1))
            fold("e", "2", 0, 2, "k2")
            for i, bank in ((2, "k0"), (3, "k3")):
                fold_b(t, q, i, 1, bank)
                fold("c", "2", i, 1, bank)
                cmp_a(q, "2", 2 * i, 2)
                fold("e", "2", i, 1, bank)
            act(T.pen[:, sl(t + 1, 512)], T.dnb[:], AF.Relu, ks("dnb", 0, 8), "pen%d" % (t + 1), "", float(t + 2), -1.0)
            mx(T.mr2[:], "mr2", "k2", 0, dq, "defs")
            if t < 3:
                act(T["u%d" % (4 - t)][:, V:W], T.tl[:, V:W], AF.Copy, "tl", "u%dg" % (4 - t), "", 0.0, float(t + 2))
            mx(T.mr2[:], "mr2", "k2", 1, T.mr2[:], "mr2")
            mx(T.mr2[:], "mr2", "k0", 0, T.mr2[:], "mr2")
            if t == 2:
                ts(T.u1[:, V:W], T.tl[:, V:W], 5.0, None, MUL, None, "tl", "u1g")
            if t == 3:
                ts(T.h0[:, V:W], T.u1[:, V:W], 255, None, AND, None, "u1g", "h0g")
            mx(T.mi[:, sl(q, 64)], "mi%d" % q, "k3", 0, T.mr2[:], "mr2")
        else:
            hops1(p)

            def paths():
                for c in range(4):
                    path_gather(t, c, "a")

            half(t, q, "2", T.mr2[:], "mr2", dq, "defs", paths, lambda: [path_shift(c) for c in range(3)])
            mx(T.mi[:, sl(q, 64)], "mi%d" % q, "k3", 0, T.mr2[:], "mr2")
            path_shift(3)
            hops2()
            hops3(t)
            back(0, 0)
            for c in range(4):
                path_put(t, p, c)

    for step in range(4):
        for c in range(2):
            s, ka, kb = sl(c, HV), ks("p0f", 2 * c, 2), "nmf%d" % c
            if step == 0:
                act(T.p0f[:, s], tab[RO][:, OWN + c * HV:OWN + (c + 1) * HV], AF.Relu, "T%d.own" % RO, ka)
            elif step == 1:
                act(T.nmf[:, s], T.p0f[:, s], AF.Ln, ka, kb, "", 2.0 ** -61, SIG)
            elif step == 2:
                act(T.p0f[:, s], T.nmf[:, s], AF.Identity, kb, ka, "", MAGIC + KD, 1.0 / A)
            else:
                act(T.nmf[:, s], T.p0f[:, s], AF.Relu, ka, kb, "", -MAGIC, 1.0)
                dma("s", T.ypath[:, s], T.nmf[:, s], "dout", kb, "")

    for j in range(1, 2 * RO):
        back(j // 2, j % 2)
    for c, (a, b) in enumerate(((0, 768), (768, 1408), (1408, 1792), (1792, V))):
        cp(T.ys[:, a:b], T.h0[:, 0:W].indirect(T.atl[:, a // 16:b // 16]), "h0g h0.0 h0.1 atl", "ys%d" % c)
        dma("s" if c % 2 == 0 else "a", T.ysum[:, a:b], T.ys[:, a:b], "dout", "ys%d" % c, "")

    wr, rd, ex, seen = {}, {}, {}, {}
    for i, o in enumerate(ops):
        dep = set(wr[k] for k in o["r"] if k in wr)
        for k in o["w"]:
            for j in ([wr[k]] if k in wr else []) + rd.get(k, []):
                if ops[j]["q"] != o["q"] or ops[j]["dma"] or o["dma"]:
                    dep.add(j)
        for k in o["x"]:
            if k in ex and ops[ex[k]]["q"] != o["q"]:
                dep.add(ex[k])
            ex[k] = i
        for k in o["r"]:
            rd.setdefault(k, []).append(i)
        for k in o["w"]:
            wr[k] = i
            rd[k] = []
        o["dsem"] = sorted(set(ops[j]["dma"] for j in dep if ops[j]["dma"]))
        o["dep"] = {}
        for j in sorted(dep):
            if not ops[j]["dma"] and seen.get((o["q"], ops[j]["q"]), -1) < j:
                o["dep"][ops[j]["q"]] = j
        for qq, j in o["dep"].items():
            seen[(o["q"], qq)] = j
            ops[j]["inc"] = True
    cnt, tot = {}, {}
    for o in ops:
        if o["dma"]:
            tot[o["dma"]] = tot.get(o["dma"], 0) + 16
        elif o.get("inc"):
            cnt[o["q"]] = cnt.get(o["q"], 0) + 1
            o["n"] = cnt[o["q"]]
    queue = {"v": g.vector, "a": g.scalar, "p": g.tensor, "g": g, "s": g.sync}
    done = set()
    for o in ops:
        e = queue[o["q"]]
        for s, val in o["ext"] + [(s, tot[s]) for s in o["dsem"]]:
            if (o["q"], s) not in done:
                done.add((o["q"], s))
                e.wait_ge(T.sem[s], val)
        for qq in sorted(o["dep"]):
            e.wait_ge(T.sem["q" + qq], ops[o["dep"][qq]]["n"])
        ins = o["fn"]()
        if o["dma"]:
            ins.then_inc(T.sem[o["dma"]], 16)
        elif o.get("inc"):
            ins.then_inc(T.sem["q" + o["q"]], 1)
    g.wait_ge(T.sem.sent, 16 * (RO - 1))
    g.sync.wait_ge(T.sem.dout, tot["dout"])
